import numpy as np
import ml_dtypes


def mxq(x, axis, fmt="e4m3"):
    dtype, down = {"e4m3": (ml_dtypes.float8_e4m3fn, 7), "e5m2": (ml_dtypes.float8_e5m2, 14)}[fmt]
    v = np.moveaxis(np.asarray(x, np.float32).astype(ml_dtypes.bfloat16).astype(np.float64), axis, -1)
    blocks = v.reshape(v.shape[:-1] + (-1, 32))
    amax = np.abs(blocks).max(-1, keepdims=True)
    byte = np.maximum(np.where(amax > 0, np.frexp(amax)[1] - 1 + 127, 0) - down, 1)
    scale = np.exp2(byte - 127.0)
    codes = (blocks / scale).astype(np.float32).astype(dtype).astype(np.float64)
    return np.moveaxis((codes * scale).reshape(v.shape), -1, axis)


WIDE = False


def mx_kscale(k):
    if not WIDE:
        return np.ones(k)
    levels = np.array([10, -10, 5, -5, 0])
    if k % 512:
        return np.exp2(np.random.permutation(np.resize(levels, k // 32))).repeat(32)
    a = np.empty((k // 512, 16))
    for p in range(k // 512):
        a[p, :8] = np.random.permutation(np.resize(levels, 8))
        for g in range(8):
            far = levels[np.abs(levels - a[p, g]) >= 10]
            a[p, g + 8] = far[np.random.randint(len(far))]
    return np.exp2(a.ravel()).repeat(32)


def f64(x):
    return np.asarray(x).astype(np.float64)


def striped(idx):
    return np.tile(idx.reshape(-1, 16).T, (8, 1)).astype(np.uint16)


def unstriped(offs):
    return offs[:16].T.reshape(-1).astype(np.int64)


def silu(v):
    return v / (1.0 + np.exp(-np.maximum(v, -700.0)))


K, T, E, C, N = 2048, 512, 4, 128, 512


def by_expert(wq, xq):
    return np.concatenate([wq[e].T @ xq[:, e * C:(e + 1) * C] for e in range(E)], axis=1)


def setup_inputs():
    n = np.random.standard_normal
    s = mx_kscale(K)[:, None]
    return {
        "xT": (n((K, T)) * s).astype(np.float32),
        "w": (n((E, K, N)) / np.sqrt(K) / s[None]).astype(np.float32),
        "b": (0.3 * n((N, E))).astype(np.float32),
        "offs": striped(np.random.permutation(T)[:E * C]),
    }


def reference(xT, w, b, offs):
    idx = unstriped(offs)
    xq = mxq(f64(xT)[:, idx], 0, "e4m3")
    y = by_expert(mxq(f64(w), 1, "e4m3"), xq)
    y = silu(y + np.repeat(f64(b), C, axis=1))
    out = np.zeros((N, T))
    out[:, idx] = y
    return out

@@ -1,0 +1,140 @@
+from contextlib import ExitStack
+
+import concourse.mybir as mybir
+
+K, T, E, C, N = 2048, 512, 4, 128, 512
+FLOPS = 2 * K * N * E * C
+
+F32 = mybir.dt.float32
+BF16 = mybir.dt.bfloat16
+U32 = mybir.dt.uint32
+U16 = mybir.dt.uint16
+U8 = mybir.dt.uint8
+FP8X4 = mybir.dt.float8_e4m3fn_x4
+SILU = mybir.ActivationFunctionType.Silu
+MULT = mybir.AluOpType.mult
+ADD = mybir.AluOpType.add
+
+P = 128
+PACK = 4
+K_PASS = P * PACK
+PASSES = K // K_PASS
+NB = N // P
+HALF = 256
+
+FS, FG = 0.75, 0.25
+X_ENGINE = {(0, 0): "v", (0, 1): "s", (1, 0): "g", (1, 1): "s", (2, 0): "g", (2, 1): "s", (3, 0): "g", (3, 1): "s"}
+W_BUFS = 10
+
+
+def cast_copy(nc, eng, out, in_):
+    if eng == "v":
+        nc.vector.tensor_copy(out=out, in_=in_)
+    elif eng == "s":
+        nc.scalar.copy(out=out, in_=in_)
+    else:
+        nc.gpsimd.tensor_scalar(out=out, in0=in_, scalar1=1.0, scalar2=0.0, op0=MULT, op1=ADD)
+
+
+def tile_routed_moe_kernel(tc, xT, w, b, offs, out):
+    nc = tc.nc
+    with ExitStack() as ctx:
+        keep = ctx.enter_context(tc.tile_pool(name="keep", bufs=1))
+        xraws = ctx.enter_context(tc.tile_pool(name="xraws", bufs=8))
+        wraws = ctx.enter_context(tc.tile_pool(name="wraws", bufs=W_BUFS))
+        stage = ctx.enter_context(tc.tile_pool(name="stage", bufs=4))
+        ypool = ctx.enter_context(tc.tile_pool(name="ypool", bufs=8))
+        psum = ctx.enter_context(tc.psum_pool(name="psum", bufs=8))
+
+        offsets = keep.tile([P, E * C // 16], U16, name="offsets")
+        nc.sync.dma_start(offsets[:], offs)
+
+        warm_in = keep.tile([P, 1], F32, name="warm_in")
+        warm_out = keep.tile([P, 1], F32, name="warm_out")
+        nc.gpsimd.memset(warm_in[:], 0.0)
+        nc.scalar.activation(out=warm_out[:], in_=warm_in[:], func=SILU)
+
+        bias = keep.tile([P, NB, E], F32, name="bias")
+        nc.scalar.dma_start(out=bias[:], in_=b.rearrange("(nb p) e -> p nb e", p=P))
+
+        x_codes = keep.tile([P, PASSES, E * C], U32, name="x_codes", align_bytes=64)
+        x_scales = keep.tile([P, PASSES, E * C], U8, name="x_scales", align_bytes=64)
+        w_codes = keep.tile([P, E * PASSES, N], U32, name="w_codes", align_bytes=64)
+        w_scales = keep.tile([P, E * PASSES, N], U8, name="w_scales", align_bytes=64)
+        windows = [keep.tile([P, T], F32, name="window%d" % nb) for nb in range(NB)]
+
+        x_view = xT.rearrange("(g p u e) n -> g u p e n", p=P, u=2, e=2)
+        x_raw = {}
+        for g in range(PASSES):
+            for u in range(2):
+                xr = xraws.tile([P, 2, T], F32, name="xr")
+                nc.sync.dma_start(out=xr[:], in_=x_view[g, u])
+                x_raw[(g, u)] = xr
+
+        for g in range(PASSES):
+            gathered = stage.tile([P, E * C, PACK], BF16, name="gathered", align_bytes=64)
+            g_words = gathered[:].rearrange("p n j -> p (n j)").bitcast(U32).rearrange("p (n u) -> p n u", u=2)
+            for u in range(2):
+                pairs = xraws.tile([P, T, 2], BF16, name="pairs")
+                cast_copy(nc, X_ENGINE[(g, u)],
+                          pairs[:].rearrange("p (c i) e -> p c e i", i=4),
+                          x_raw[(g, u)][:].rearrange("p e (c i) -> p c e i", i=4))
+                window = pairs[:].rearrange("p n e -> p (n e)").bitcast(U32)
+                for h in range(E * C // HALF):
+                    nc.vector.tensor_copy(
+                        out=g_words[:, h * HALF:(h + 1) * HALF, u],
+                        in_=window.indirect(offsets[:, h * HALF // 16:(h + 1) * HALF // 16]),
+                    )
+            nc.vector.quantize_mx(
+                out=x_codes[:, g, :].bitcast(FP8X4),
+                scales=x_scales[:, g, :],
+                in_=gathered[:].rearrange("p n j -> p (n j)"),
+            )
+
+        chunks = []
+        for e in range(E - 1):
+            for g in range(PASSES):
+                chunks.append((e, g, 0, N))
+        for c0 in range(0, N, N // 2):
+            for g in range(PASSES):
+                chunks.append((E - 1, g, c0, c0 + N // 2))
+
+        acc = {}
+        for (e, g, c0, c1) in chunks:
+            c = e * PASSES + g
+            width = c1 - c0
+            raw = wraws.tile([P, PACK, width], F32, name="raw")
+            nc.sync.dma_start(out=raw[:], in_=w[e, g * K_PASS:(g + 1) * K_PASS, c0:c1].rearrange("(p j) n -> p j n", j=PACK))
+            grouped = stage.tile([P, width, PACK], BF16, name="grouped", align_bytes=64)
+            s_end = int(width * FS) // 8 * 8
+            g_end = s_end + int(width * FG) // 8 * 8
+            for eng, a, z in (("s", 0, s_end), ("g", s_end, g_end), ("v", g_end, width)):
+                if z > a:
+                    cast_copy(nc, eng,
+                              grouped[:, a:z, :].rearrange("p (c i) t -> p c t i", i=4),
+                              raw[:, :, a:z].rearrange("p t (c i) -> p c t i", i=4))
+            nc.vector.quantize_mx(
+                out=w_codes[:, c, c0:c1].bitcast(FP8X4),
+                scales=w_scales[:, c, c0:c1],
+                in_=grouped[:].rearrange("p n j -> p (n j)"),
+            )
+            for nb in range(c0 // P, c1 // P):
+                if g == 0:
+                    acc[(e, nb)] = psum.tile([P, C], F32, name="acc")
+                nc.tensor.matmul_mx(
+                    out=acc[(e, nb)][:],
+                    lhsT=w_codes[:, c, nb * P:(nb + 1) * P].bitcast(FP8X4),
+                    lhsT_scale=w_scales[:, c, nb * P:(nb + 1) * P],
+                    rhs=x_codes[:, g, e * C:(e + 1) * C].bitcast(FP8X4),
+                    rhs_scale=x_scales[:, g, e * C:(e + 1) * C],
+                    start=(g == 0),
+                    stop=(g == PASSES - 1),
+                )
+            if g == PASSES - 1:
+                for nb in range(c0 // P, c1 // P):
+                    y = ypool.tile([P, C], F32, name="y")
+                    nc.scalar.activation(out=y[:], in_=acc[(e, nb)][:], func=SILU, bias=bias[:, nb, e:e + 1], scale=1.0)
+                    nc.vector.tensor_copy(windows[nb][:].indirect(offsets[:, e * C // 16:(e + 1) * C // 16]), y[:])
+
+        for nb in range(NB):
+            nc.sync.dma_start(out=out[nb * P:(nb + 1) * P, :], in_=windows[nb][:])

@@ -95,9 +95,12 @@ def tile_routed_moe_kernel(tc, xT, w, b, offs, out):
         for e in range(E - 1):
             for g in range(PASSES):
                 chunks.append((e, g, 0, N))
-        for c0 in range(0, N, N // 2):
-            for g in range(PASSES):
-                chunks.append((E - 1, g, c0, c0 + N // 2))
+        for g in range(PASSES):
+            chunks.append((E - 1, g, 0, N // 2))
+        for g in range(PASSES - 1):
+            chunks.append((E - 1, g, N // 2, N))
+        for c0 in range(N // 2, N, P):
+            chunks.append((E - 1, PASSES - 1, c0, c0 + P))
 
         acc = {}
         for (e, g, c0, c1) in chunks:

@@ -65,11 +65,15 @@ def tile_routed_moe_kernel(tc, xT, w, b, offs, out):
 
         x_view = xT.rearrange("(g p u e) n -> g u p e n", p=P, u=2, e=2)
         x_raw = {}
+        early_raw = {}
         for g in range(PASSES):
             for u in range(2):
                 xr = xraws.tile([P, 2, T], F32, name="xr")
                 nc.sync.dma_start(out=xr[:], in_=x_view[g, u])
                 x_raw[(g, u)] = xr
+            raw = wraws.tile([P, PACK, N], F32, name="raw")
+            nc.sync.dma_start(out=raw[:], in_=w[0, g * K_PASS:(g + 1) * K_PASS, :].rearrange("(p j) n -> p j n", j=PACK))
+            early_raw[g] = raw
 
         for g in range(PASSES):
             gathered = stage.tile([P, E * C, PACK], BF16, name="gathered", align_bytes=64)
@@ -106,8 +110,11 @@ def tile_routed_moe_kernel(tc, xT, w, b, offs, out):
         for (e, g, c0, c1) in chunks:
             c = e * PASSES + g
             width = c1 - c0
-            raw = wraws.tile([P, PACK, width], F32, name="raw")
-            nc.sync.dma_start(out=raw[:], in_=w[e, g * K_PASS:(g + 1) * K_PASS, c0:c1].rearrange("(p j) n -> p j n", j=PACK))
+            if e == 0:
+                raw = early_raw[g]
+            else:
+                raw = wraws.tile([P, PACK, width], F32, name="raw")
+                nc.sync.dma_start(out=raw[:], in_=w[e, g * K_PASS:(g + 1) * K_PASS, c0:c1].rearrange("(p j) n -> p j n", j=PACK))
             grouped = stage.tile([P, width, PACK], BF16, name="grouped", align_bytes=64)
             s_end = int(width * FS) // 8 * 8
             g_end = s_end + int(width * FG) // 8 * 8

@@ -22,8 +22,13 @@ PASSES = K // K_PASS
 NB = N // P
 HALF = 256
 
-FS, FG = 0.75, 0.25
-X_ENGINE = {(0, 0): "v", (0, 1): "s", (1, 0): "g", (1, 1): "s", (2, 0): "g", (2, 1): "s", (3, 0): "g", (3, 1): "s"}
+def splits(e, g, c0, width):
+    if (e, g) == (E - 2, PASSES - 1):
+        return width // 2, width // 2
+    return width * 3 // 4, width
+
+
+X_ENGINE = {(0, 0): "v", (0, 1): "s", (1, 0): "s", (1, 1): "s", (2, 0): "s", (2, 1): "s", (3, 0): "g", (3, 1): "s"}
 W_BUFS = 10
 
 
@@ -115,36 +120,38 @@ def tile_routed_moe_kernel(tc, xT, w, b, offs, out):
             else:
                 raw = wraws.tile([P, PACK, width], F32, name="raw")
                 nc.sync.dma_start(out=raw[:], in_=w[e, g * K_PASS:(g + 1) * K_PASS, c0:c1].rearrange("(p j) n -> p j n", j=PACK))
-            grouped = stage.tile([P, width, PACK], BF16, name="grouped", align_bytes=64)
-            s_end = int(width * FS) // 8 * 8
-            g_end = s_end + int(width * FG) // 8 * 8
-            for eng, a, z in (("s", 0, s_end), ("g", s_end, g_end), ("v", g_end, width)):
-                if z > a:
-                    cast_copy(nc, eng,
-                              grouped[:, a:z, :].rearrange("p (c i) t -> p c t i", i=4),
-                              raw[:, :, a:z].rearrange("p t (c i) -> p c t i", i=4))
-            nc.vector.quantize_mx(
-                out=w_codes[:, c, c0:c1].bitcast(FP8X4),
-                scales=w_scales[:, c, c0:c1],
-                in_=grouped[:].rearrange("p n j -> p (n j)"),
-            )
-            for nb in range(c0 // P, c1 // P):
-                if g == 0:
-                    acc[(e, nb)] = psum.tile([P, C], F32, name="acc")
-                nc.tensor.matmul_mx(
-                    out=acc[(e, nb)][:],
-                    lhsT=w_codes[:, c, nb * P:(nb + 1) * P].bitcast(FP8X4),
-                    lhsT_scale=w_scales[:, c, nb * P:(nb + 1) * P],
-                    rhs=x_codes[:, g, e * C:(e + 1) * C].bitcast(FP8X4),
-                    rhs_scale=x_scales[:, g, e * C:(e + 1) * C],
-                    start=(g == 0),
-                    stop=(g == PASSES - 1),
+            pieces = [(0, N // 2), (N // 2, N)] if (e, g) == (E - 2, PASSES - 1) else [(0, width)]
+            for (r0, r1) in pieces:
+                pw = r1 - r0
+                grouped = stage.tile([P, pw, PACK], BF16, name="grouped", align_bytes=64)
+                s_end, g_end = splits(e, g, c0, pw)
+                for eng, a, z in (("s", 0, s_end), ("g", s_end, g_end), ("v", g_end, pw)):
+                    if z > a:
+                        cast_copy(nc, eng,
+                                  grouped[:, a:z, :].rearrange("p (c i) t -> p c t i", i=4),
+                                  raw[:, :, r0 + a:r0 + z].rearrange("p t (c i) -> p c t i", i=4))
+                nc.vector.quantize_mx(
+                    out=w_codes[:, c, c0 + r0:c0 + r1].bitcast(FP8X4),
+                    scales=w_scales[:, c, c0 + r0:c0 + r1],
+                    in_=grouped[:].rearrange("p n j -> p (n j)"),
                 )
-            if g == PASSES - 1:
-                for nb in range(c0 // P, c1 // P):
-                    y = ypool.tile([P, C], F32, name="y")
-                    nc.scalar.activation(out=y[:], in_=acc[(e, nb)][:], func=SILU, bias=bias[:, nb, e:e + 1], scale=1.0)
-                    nc.vector.tensor_copy(windows[nb][:].indirect(offsets[:, e * C // 16:(e + 1) * C // 16]), y[:])
+                for nb in range((c0 + r0) // P, (c0 + r1) // P):
+                    if g == 0:
+                        acc[(e, nb)] = psum.tile([P, C], F32, name="acc")
+                    nc.tensor.matmul_mx(
+                        out=acc[(e, nb)][:],
+                        lhsT=w_codes[:, c, nb * P:(nb + 1) * P].bitcast(FP8X4),
+                        lhsT_scale=w_scales[:, c, nb * P:(nb + 1) * P],
+                        rhs=x_codes[:, g, e * C:(e + 1) * C].bitcast(FP8X4),
+                        rhs_scale=x_scales[:, g, e * C:(e + 1) * C],
+                        start=(g == 0),
+                        stop=(g == PASSES - 1),
+                    )
+                if g == PASSES - 1:
+                    for nb in range((c0 + r0) // P, (c0 + r1) // P):
+                        y = ypool.tile([P, C], F32, name="y")
+                        nc.scalar.activation(out=y[:], in_=acc[(e, nb)][:], func=SILU, bias=bias[:, nb, e:e + 1], scale=1.0)
+                        nc.vector.tensor_copy(windows[nb][:].indirect(offsets[:, e * C // 16:(e + 1) * C // 16]), y[:])
 
         for nb in range(NB):
             nc.sync.dma_start(out=out[nb * P:(nb + 1) * P, :], in_=windows[nb][:])

from contextlib import ExitStack

import concourse.mybir as mybir

K, T, E, C, N = 2048, 512, 4, 128, 512
FLOPS = 2 * K * N * E * C

F32 = mybir.dt.float32
BF16 = mybir.dt.bfloat16
U32 = mybir.dt.uint32
U16 = mybir.dt.uint16
U8 = mybir.dt.uint8
FP8X4 = mybir.dt.float8_e4m3fn_x4
SILU = mybir.ActivationFunctionType.Silu
MULT = mybir.AluOpType.mult
ADD = mybir.AluOpType.add

P = 128
PACK = 4
K_PASS = P * PACK
PASSES = K // K_PASS
NB = N // P
HALF = 256

def splits(e, g, c0, width):
    if (e, g) == (E - 2, PASSES - 1):
        return width // 2, width // 2
    return width * 3 // 4, width


X_ENGINE = {(0, 0): "v", (0, 1): "s", (1, 0): "s", (1, 1): "s", (2, 0): "s", (2, 1): "s", (3, 0): "g", (3, 1): "s"}
W_BUFS = 10


def cast_copy(nc, eng, out, in_):
    if eng == "v":
        nc.vector.tensor_copy(out=out, in_=in_)
    elif eng == "s":
        nc.scalar.copy(out=out, in_=in_)
    else:
        nc.gpsimd.tensor_scalar(out=out, in0=in_, scalar1=1.0, scalar2=0.0, op0=MULT, op1=ADD)


def tile_routed_moe_kernel(tc, xT, w, b, offs, out):
    nc = tc.nc
    with ExitStack() as ctx:
        keep = ctx.enter_context(tc.tile_pool(name="keep", bufs=1))
        xraws = ctx.enter_context(tc.tile_pool(name="xraws", bufs=8))
        wraws = ctx.enter_context(tc.tile_pool(name="wraws", bufs=W_BUFS))
        stage = ctx.enter_context(tc.tile_pool(name="stage", bufs=4))
        ypool = ctx.enter_context(tc.tile_pool(name="ypool", bufs=8))
        psum = ctx.enter_context(tc.psum_pool(name="psum", bufs=8))

        offsets = keep.tile([P, E * C // 16], U16, name="offsets")
        nc.sync.dma_start(offsets[:], offs)

        warm_in = keep.tile([P, 1], F32, name="warm_in")
        warm_out = keep.tile([P, 1], F32, name="warm_out")
        nc.gpsimd.memset(warm_in[:], 0.0)
        nc.scalar.activation(out=warm_out[:], in_=warm_in[:], func=SILU)

        bias = keep.tile([P, NB, E], F32, name="bias")
        nc.scalar.dma_start(out=bias[:], in_=b.rearrange("(nb p) e -> p nb e", p=P))

        x_codes = keep.tile([P, PASSES, E * C], U32, name="x_codes", align_bytes=64)
        x_scales = keep.tile([P, PASSES, E * C], U8, name="x_scales", align_bytes=64)
        w_codes = keep.tile([P, E * PASSES, N], U32, name="w_codes", align_bytes=64)
        w_scales = keep.tile([P, E * PASSES, N], U8, name="w_scales", align_bytes=64)
        windows = [keep.tile([P, T], F32, name="window%d" % nb) for nb in range(NB)]

        x_view = xT.rearrange("(g p u e) n -> g u p e n", p=P, u=2, e=2)
        x_raw = {}
        early_raw = {}
        for g in range(PASSES):
            for u in range(2):
                xr = xraws.tile([P, 2, T], F32, name="xr")
                nc.sync.dma_start(out=xr[:], in_=x_view[g, u])
                x_raw[(g, u)] = xr
            raw = wraws.tile([P, PACK, N], F32, name="raw")
            nc.sync.dma_start(out=raw[:], in_=w[0, g * K_PASS:(g + 1) * K_PASS, :].rearrange("(p j) n -> p j n", j=PACK))
            early_raw[g] = raw

        for g in range(PASSES):
            gathered = stage.tile([P, E * C, PACK], BF16, name="gathered", align_bytes=64)
            g_words = gathered[:].rearrange("p n j -> p (n j)").bitcast(U32).rearrange("p (n u) -> p n u", u=2)
            for u in range(2):
                pairs = xraws.tile([P, T, 2], BF16, name="pairs")
                cast_copy(nc, X_ENGINE[(g, u)],
                          pairs[:].rearrange("p (c i) e -> p c e i", i=4),
                          x_raw[(g, u)][:].rearrange("p e (c i) -> p c e i", i=4))
                window = pairs[:].rearrange("p n e -> p (n e)").bitcast(U32)
                for h in range(E * C // HALF):
                    nc.vector.tensor_copy(
                        out=g_words[:, h * HALF:(h + 1) * HALF, u],
                        in_=window.indirect(offsets[:, h * HALF // 16:(h + 1) * HALF // 16]),
                    )
            nc.vector.quantize_mx(
                out=x_codes[:, g, :].bitcast(FP8X4),
                scales=x_scales[:, g, :],
                in_=gathered[:].rearrange("p n j -> p (n j)"),
            )

        chunks = []
        for e in range(E - 1):
            for g in range(PASSES):
                chunks.append((e, g, 0, N))
        for g in range(PASSES):
            chunks.append((E - 1, g, 0, N // 2))
        for g in range(PASSES - 1):
            chunks.append((E - 1, g, N // 2, N))
        for c0 in range(N // 2, N, P):
            chunks.append((E - 1, PASSES - 1, c0, c0 + P))

        acc = {}
        for (e, g, c0, c1) in chunks:
            c = e * PASSES + g
            width = c1 - c0
            if e == 0:
                raw = early_raw[g]
            else:
                raw = wraws.tile([P, PACK, width], F32, name="raw")
                nc.sync.dma_start(out=raw[:], in_=w[e, g * K_PASS:(g + 1) * K_PASS, c0:c1].rearrange("(p j) n -> p j n", j=PACK))
            pieces = [(0, N // 2), (N // 2, N)] if (e, g) == (E - 2, PASSES - 1) else [(0, width)]
            for (r0, r1) in pieces:
                pw = r1 - r0
                grouped = stage.tile([P, pw, PACK], BF16, name="grouped", align_bytes=64)
                s_end, g_end = splits(e, g, c0, pw)
                for eng, a, z in (("s", 0, s_end), ("g", s_end, g_end), ("v", g_end, pw)):
                    if z > a:
                        cast_copy(nc, eng,
                                  grouped[:, a:z, :].rearrange("p (c i) t -> p c t i", i=4),
                                  raw[:, :, r0 + a:r0 + z].rearrange("p t (c i) -> p c t i", i=4))
                nc.vector.quantize_mx(
                    out=w_codes[:, c, c0 + r0:c0 + r1].bitcast(FP8X4),
                    scales=w_scales[:, c, c0 + r0:c0 + r1],
                    in_=grouped[:].rearrange("p n j -> p (n j)"),
                )
                for nb in range((c0 + r0) // P, (c0 + r1) // P):
                    if g == 0:
                        acc[(e, nb)] = psum.tile([P, C], F32, name="acc")
                    nc.tensor.matmul_mx(
                        out=acc[(e, nb)][:],
                        lhsT=w_codes[:, c, nb * P:(nb + 1) * P].bitcast(FP8X4),
                        lhsT_scale=w_scales[:, c, nb * P:(nb + 1) * P],
                        rhs=x_codes[:, g, e * C:(e + 1) * C].bitcast(FP8X4),
                        rhs_scale=x_scales[:, g, e * C:(e + 1) * C],
                        start=(g == 0),
                        stop=(g == PASSES - 1),
                    )
                if g == PASSES - 1:
                    for nb in range((c0 + r0) // P, (c0 + r1) // P):
                        y = ypool.tile([P, C], F32, name="y")
                        nc.scalar.activation(out=y[:], in_=acc[(e, nb)][:], func=SILU, bias=bias[:, nb, e:e + 1], scale=1.0)
                        nc.vector.tensor_copy(windows[nb][:].indirect(offsets[:, e * C // 16:(e + 1) * C // 16]), y[:])

        for nb in range(NB):
            nc.sync.dma_start(out=out[nb * P:(nb + 1) * P, :], in_=windows[nb][:])
